import numpy as np
import ml_dtypes


def mxq(x, axis, fmt="e4m3"):
    dtype, down = {"e4m3": (ml_dtypes.float8_e4m3fn, 7), "e5m2": (ml_dtypes.float8_e5m2, 14)}[fmt]
    v = np.moveaxis(np.asarray(x, np.float32).astype(ml_dtypes.bfloat16).astype(np.float64), axis, -1)
    blocks = v.reshape(v.shape[:-1] + (-1, 32))
    amax = np.abs(blocks).max(-1, keepdims=True)
    byte = np.maximum(np.where(amax > 0, np.frexp(amax)[1] - 1 + 127, 0) - down, 1)
    scale = np.exp2(byte - 127.0)
    codes = (blocks / scale).astype(np.float32).astype(dtype).astype(np.float64)
    return np.moveaxis((codes * scale).reshape(v.shape), -1, axis)


WIDE = False


def mx_kscale(k):
    if not WIDE:
        return np.ones(k)
    levels = np.array([10, -10, 5, -5, 0])
    if k % 512:
        return np.exp2(np.random.permutation(np.resize(levels, k // 32))).repeat(32)
    a = np.empty((k // 512, 16))
    for p in range(k // 512):
        a[p, :8] = np.random.permutation(np.resize(levels, 8))
        for g in range(8):
            far = levels[np.abs(levels - a[p, g]) >= 10]
            a[p, g + 8] = far[np.random.randint(len(far))]
    return np.exp2(a.ravel()).repeat(32)


def f64(x):
    return np.asarray(x).astype(np.float64)


def striped(idx):
    return np.tile(idx.reshape(-1, 16).T, (8, 1)).astype(np.uint16)


def unstriped(offs):
    return offs[:16].T.reshape(-1).astype(np.int64)


def pack_weight(w):
    k, n = w.shape
    w = f64(np.asarray(w, np.float32).astype(ml_dtypes.bfloat16)).reshape(k // 32, 32, n)
    amax = np.abs(w).max(1)
    byte = np.clip(np.where(amax > 0, np.frexp(amax)[1] - 1 + 127 - 7, 1), 1, 254)
    scaled = (w * np.exp2(127.0 - byte)[:, None, :]).reshape(k, n).astype(np.float32)
    words = np.ascontiguousarray(scaled.reshape(k // 512, 128, 4, n).transpose(0, 1, 3, 2)).astype(ml_dtypes.float8_e4m3fn).view(np.uint8)
    return words, np.ascontiguousarray(byte.astype(np.uint8).reshape(k // 512, 16, n))


def unpack_weight(words, scales):
    g, p, n, _ = words.shape
    vals = np.ascontiguousarray(words).view(ml_dtypes.float8_e4m3fn).astype(np.float64) * np.repeat(np.exp2(scales.astype(np.float64) - 127.0), 8, axis=1)[..., None]
    return vals.transpose(0, 1, 3, 2).reshape(g * 512, n)


K, T, E, C, N = 1536, 768, 6, 256, 384


def by_expert(wq, xq):
    return np.concatenate([wq[e].T @ xq[:, e * C:(e + 1) * C] for e in range(E)], axis=1)


def setup_inputs():
    n = np.random.standard_normal
    s = mx_kscale(K)[:, None]
    first = np.random.permutation(np.repeat(np.arange(E), T // E))
    second = (first + 1 + np.random.permutation(np.repeat(np.arange(E - 1), -(-T // (E - 1)))[:T])) % E
    while np.bincount(second, minlength=E).max() != T // E:
        load = np.bincount(second, minlength=E); hi, lo = int(load.argmax()), int(load.argmin())
        t = np.flatnonzero((second == hi) & (first != lo))[0]; second[t] = lo
    slot_token = np.empty(E * C, np.int64); pos = np.empty((2, T), np.int64); fill = np.zeros(E, np.int64)
    place = np.stack([np.random.permutation(C) for _ in range(E)])
    for r, deal in enumerate((first, second)):
        for t in np.random.permutation(T):
            e = deal[t]; j = e * C + place[e, fill[e]]; fill[e] += 1; slot_token[j] = t; pos[r, t] = j
    g = np.random.uniform(0.2, 0.8, T)
    packed = [pack_weight(m) for m in n((E, K, N)) / np.sqrt(K) / s[None]]
    return {
        "xT": (n((K, T)) * s).astype(np.float32),
        "w_words": np.stack([m[0] for m in packed]),
        "w_scales": np.stack([m[1] for m in packed]),
        "gate": np.stack([np.tile(g, (N, 1)), np.tile(1.0 - g, (N, 1))]).astype(np.float32),
        "offs": striped(slot_token),
        "pos1": striped(pos[0]),
        "pos2": striped(pos[1]),
    }


def reference(xT, w_words, w_scales, gate, offs, pos1, pos2):
    idx = unstriped(offs)
    xq = mxq(f64(xT)[:, idx], 0, "e4m3")
    w = np.stack([unpack_weight(w_words[e], w_scales[e]) for e in range(E)])
    y = by_expert(w, xq)
    return f64(gate[0]) * y[:, unstriped(pos1)] + f64(gate[1]) * y[:, unstriped(pos2)]

@@ -1,0 +1,176 @@
+from contextlib import ExitStack
+
+import concourse.mybir as mybir
+from concourse.masks import make_identity
+
+K, T, E, C, N = 1536, 768, 6, 256, 384
+FLOPS = 2 * K * E * C * N
+
+F32 = mybir.dt.float32
+BF16 = mybir.dt.bfloat16
+I32 = mybir.dt.int32
+U32 = mybir.dt.uint32
+U16 = mybir.dt.uint16
+U8 = mybir.dt.uint8
+FP8X4 = mybir.dt.float8_e4m3fn_x4
+MULT = mybir.AluOpType.mult
+ADD = mybir.AluOpType.add
+
+P = 128
+A = K // 512
+M = N // P
+CHUNK = 256
+W = 2048
+PIECE = 512
+S = E * C // PIECE
+
+
+def tile_routed_moe_kernel(tc, xT, w_words, w_scales, gate, offs, pos1, pos2, out):
+    nc = tc.nc
+    with ExitStack() as ctx:
+        keep = ctx.enter_context(tc.tile_pool(name="keep", bufs=1))
+        psum = ctx.enter_context(tc.psum_pool(name="psum", bufs=8))
+
+        offs_t = keep.tile([P, E * C // 16], U16, name="offs_t")
+        pos1_t = keep.tile([P, T // 16], U16, name="pos1_t")
+        pos2_t = keep.tile([P, T // 16], U16, name="pos2_t")
+        w_planes = keep.tile([P, E * A, N], U8, name="w_planes", align_bytes=64)
+        tok_bytes = keep.tile([P, T], U8, name="tok_bytes", align_bytes=64)
+        slot_bytes = keep.tile([P, E * C], U8, name="slot_bytes", align_bytes=64)
+        ident = keep.tile([P, P], F32, name="ident")
+
+        nc.vector.memset(w_planes[:].rearrange("p g n -> p (g n)").bitcast(I32), 0)
+        nc.gpsimd.memset(tok_bytes[:], 0)
+        make_identity(nc, ident[:])
+
+        x_view = xT.rearrange("(a p j) t -> a p j t", p=P, j=4)
+        raw = {}
+        for a in range(A):
+            for c in range(T // CHUNK):
+                raw[a, c] = keep.tile([P, 4, CHUNK], F32, name=f"raw{a}_{c}")
+                nc.sync.dma_start(raw[a, c][:], x_view[a][:, :, c * CHUNK : (c + 1) * CHUNK])
+            if a == 0:
+                nc.sync.dma_start(offs_t[:], offs)
+        for q in range(4):
+            nc.sync.dma_start(
+                w_planes[32 * q : 32 * q + 4].bitcast(I32),
+                w_scales.rearrange("e a q n -> q (e a) n")[4 * q : 4 * q + 4].bitcast(I32),
+            )
+        w = []
+        for e in range(E):
+            w_e = keep.tile([P, A, N], U32, name=f"w{e}", align_bytes=64)
+            nc.sync.dma_start(w_e[:].bitcast(I32), w_words[e].rearrange("a p n t -> p a (n t)").bitcast(I32))
+            w.append(w_e)
+        nc.sync.dma_start(pos1_t[:], pos1)
+        nc.sync.dma_start(pos2_t[:], pos2)
+        gates = []
+        for m in range(M):
+            gate_m = keep.tile([P, 2, T], F32, name=f"gate{m}")
+            nc.sync.dma_start(gate_m[:], gate[:, m * P : (m + 1) * P, :].rearrange("g p t -> p g t"))
+            gates.append(gate_m)
+
+        tok_words, slot_words, x_bf = [], [], []
+        for a in range(A):
+            tok_words.append(keep.tile([P, W], U32, name=f"tok_words{a}", align_bytes=64))
+            slot_words.append(keep.tile([P, E * C], U32, name=f"slot_words{a}", align_bytes=64))
+            x_bf.append(keep.tile([P, T, 4], BF16, name=f"x_bf{a}", align_bytes=64))
+        y = []
+        for m in range(M):
+            y.append(keep.tile([P, E * C], F32, name=f"y{m}"))
+
+        def interleave(a, c, share):
+            base = c * CHUNK
+            src = raw[a, c][:].rearrange("p j t -> p t j")
+            if share > 0:
+                nc.vector.tensor_copy(x_bf[a][:, base : base + share, :], src[:, :share, :])
+            if share < CHUNK:
+                nc.scalar.copy(x_bf[a][:, base + share : base + CHUNK, :], src[:, share:, :])
+
+        def quantise(a, t0, t1):
+            nc.vector.quantize_mx(
+                out=tok_words[a][:, t0:t1].bitcast(FP8X4),
+                scales=tok_bytes[4 * a : P, t0:t1],
+                in_=x_bf[a][:, t0:t1, :].rearrange("p t j -> p (t j)"),
+            )
+
+        def piece_offsets(s):
+            return offs_t[:, s * PIECE // 16 : (s + 1) * PIECE // 16]
+
+        def gather_words(a, s):
+            nc.vector.tensor_copy(
+                slot_words[a][:, s * PIECE : (s + 1) * PIECE], tok_words[a][:].indirect(piece_offsets(s))
+            )
+
+        def gather_bytes(s):
+            nc.vector.tensor_copy(slot_bytes[:, s * PIECE : (s + 1) * PIECE], tok_bytes[:].indirect(piece_offsets(s)))
+
+        def multiply(acc, m, e, a):
+            slots = slice(e * C, (e + 1) * C)
+            rows = slice(m * P, (m + 1) * P)
+            nc.tensor.matmul_mx(
+                out=acc,
+                lhsT=w[e][:, a, rows].bitcast(FP8X4),
+                lhsT_scale=w_planes[:, e * A + a, rows],
+                rhs=slot_words[a][:, slots].bitcast(FP8X4),
+                rhs_scale=slot_bytes[4 * a : P, slots],
+                start=(a == 0),
+                stop=(a == A - 1),
+            )
+
+        def pair(s):
+            for m in range(M):
+                acc = psum.tile([P, PIECE], F32, name="acc")
+                for h in range(2):
+                    for a in range(A):
+                        multiply(acc[:, h * C : (h + 1) * C], m, 2 * s + h, a)
+                nc.scalar.copy(y[m][:, s * PIECE : (s + 1) * PIECE], acc[:])
+
+        for a in range(A):
+            for c in range(T // CHUNK):
+                interleave(a, c, (256, 96, 128)[c] if a == 0 else 0)
+            quantise(a, 0, 512)
+            quantise(a, 512, 768)
+            if a < A - 1:
+                nc.vector.tensor_copy(slot_words[a][:], tok_words[a][:].indirect(offs_t[:]))
+        gather_bytes(0)
+        gather_words(2, 0)
+        pair(0)
+        gather_bytes(1)
+        gather_words(2, 1)
+        pair(1)
+        gather_bytes(2)
+        gather_words(2, 2)
+        last = {}
+        for m in range(M):
+            for e in (4, 5):
+                last[m, e] = psum.tile([P, PIECE], F32, name="acc")
+                for a in range(A - 1):
+                    multiply(last[m, e][:, :C], m, e, a)
+        for m in range(M):
+            for e in (4, 5):
+                multiply(last[m, e][:, :C], m, e, A - 1)
+            nc.scalar.copy(y[m][:, 4 * C : 5 * C], last[m, 4][:, :C])
+            if m == 0:
+                nc.vector.tensor_copy(y[m][:, 5 * C : 6 * C], last[m, 5][:, :C])
+            else:
+                nc.scalar.copy(y[m][:, 5 * C : 6 * C], last[m, 5][:, :C])
+
+        for m in range(M):
+            rows = slice(m * P, (m + 1) * P)
+            first = keep.tile([P, T], F32, name=f"first{m}")
+            nc.vector.tensor_tensor(first[:], y[m][:].indirect(pos1_t[:]), gates[m][:, 0, :], MULT)
+            for t0, t1 in ((0, 512), (512, 768)) if m < M - 1 else ((0, 256), (256, 512), (512, 768)):
+                n = t1 - t0
+                second = keep.tile([P, n], F32, name=f"second{m}_{t0}")
+                nc.vector.tensor_tensor(
+                    second[:], y[m][:].indirect(pos2_t[:, t0 // 16 : t1 // 16]), gates[m][:, 1, t0:t1], MULT
+                )
+                result = keep.tile([P, n], F32, name=f"result{m}_{t0}")
+                if m == M - 1 and t0 == 512:
+                    nc.vector.tensor_tensor(result[:], first[:, t0:t1], second[:], ADD)
+                else:
+                    acc = psum.tile([P, PIECE], F32, name="acc")
+                    nc.tensor.matmul(acc[:, :n], ident[:], first[:, t0:t1], start=True, stop=False)
+                    nc.tensor.matmul(acc[:, :n], ident[:], second[:], start=False, stop=True)
+                    nc.scalar.copy(result[:], acc[:, :n])
+                nc.sync.dma_start(out[rows, t0:t1], result[:])

@@ -35,12 +35,12 @@ def tile_routed_moe_kernel(tc, xT, w_words, w_scales, gate, offs, pos1, pos2, ou
         pos1_t = keep.tile([P, T // 16], U16, name="pos1_t")
         pos2_t = keep.tile([P, T // 16], U16, name="pos2_t")
         w_planes = keep.tile([P, E * A, N], U8, name="w_planes", align_bytes=64)
-        tok_bytes = keep.tile([P, T], U8, name="tok_bytes", align_bytes=64)
+        tok_bytes = keep.tile([P, W], U8, name="tok_bytes", align_bytes=64)
         slot_bytes = keep.tile([P, E * C], U8, name="slot_bytes", align_bytes=64)
         ident = keep.tile([P, P], F32, name="ident")
 
         nc.vector.memset(w_planes[:].rearrange("p g n -> p (g n)").bitcast(I32), 0)
-        nc.gpsimd.memset(tok_bytes[:], 0)
+        nc.gpsimd.memset(tok_bytes[:, :T], 0)
         make_identity(nc, ident[:])
 
         x_view = xT.rearrange("(a p j) t -> a p j t", p=P, j=4)
@@ -65,9 +65,10 @@ def tile_routed_moe_kernel(tc, xT, w_words, w_scales, gate, offs, pos1, pos2, ou
         nc.sync.dma_start(pos2_t[:], pos2)
         gates = []
         for m in range(M):
-            gate_m = keep.tile([P, 2, T], F32, name=f"gate{m}")
-            nc.sync.dma_start(gate_m[:], gate[:, m * P : (m + 1) * P, :].rearrange("g p t -> p g t"))
-            gates.append(gate_m)
+            for g in range(2):
+                gate_mg = keep.tile([P, T], F32, name=f"gate{m}_{g}")
+                nc.sync.dma_start(gate_mg[:], gate[g, m * P : (m + 1) * P, :])
+                gates.append(gate_mg)
 
         tok_words, slot_words, x_bf = [], [], []
         for a in range(A):
@@ -93,16 +94,8 @@ def tile_routed_moe_kernel(tc, xT, w_words, w_scales, gate, offs, pos1, pos2, ou
                 in_=x_bf[a][:, t0:t1, :].rearrange("p t j -> p (t j)"),
             )
 
-        def piece_offsets(s):
-            return offs_t[:, s * PIECE // 16 : (s + 1) * PIECE // 16]
-
-        def gather_words(a, s):
-            nc.vector.tensor_copy(
-                slot_words[a][:, s * PIECE : (s + 1) * PIECE], tok_words[a][:].indirect(piece_offsets(s))
-            )
-
-        def gather_bytes(s):
-            nc.vector.tensor_copy(slot_bytes[:, s * PIECE : (s + 1) * PIECE], tok_bytes[:].indirect(piece_offsets(s)))
+        def gather(dst, window, j0, j1):
+            nc.vector.tensor_copy(dst[:, j0:j1], window[:].indirect(offs_t[:, j0 // 16 : j1 // 16]))
 
         def multiply(acc, m, e, a):
             slots = slice(e * C, (e + 1) * C)
@@ -117,60 +110,54 @@ def tile_routed_moe_kernel(tc, xT, w_words, w_scales, gate, offs, pos1, pos2, ou
                 stop=(a == A - 1),
             )
 
-        def pair(s):
-            for m in range(M):
+        for a in range(A):
+            for c in range(T // CHUNK):
+                interleave(a, c, (256, 96, 160)[c] if a == 0 else 0)
+            quantise(a, 0, 512)
+            quantise(a, 512, 768)
+            if a < A - 1:
+                gather(slot_words[a], tok_words[a], 0, E * C)
+        gather(slot_bytes, tok_bytes, 0, E * C)
+        gather(slot_words[2], tok_words[2], 0, 4 * C)
+        gather(slot_words[2], tok_words[2], 4 * C, 6 * C)
+
+        accs = []
+        for e in range(E):
+            acc = psum.tile([P, PIECE], F32, name="acc")
+            for a in range(A - 1):
+                multiply(acc[:, :C], 0, e, a)
+            accs.append(acc)
+        for e in range(E):
+            multiply(accs[e][:, :C], 0, e, A - 1)
+            if e == E - 1:
+                nc.vector.tensor_copy(y[0][:, e * C : (e + 1) * C], accs[e][:, :C])
+            else:
+                nc.scalar.copy(y[0][:, e * C : (e + 1) * C], accs[e][:, :C])
+        for m in range(1, M):
+            for s in range(S):
                 acc = psum.tile([P, PIECE], F32, name="acc")
                 for h in range(2):
                     for a in range(A):
                         multiply(acc[:, h * C : (h + 1) * C], m, 2 * s + h, a)
                 nc.scalar.copy(y[m][:, s * PIECE : (s + 1) * PIECE], acc[:])
 
-        for a in range(A):
-            for c in range(T // CHUNK):
-                interleave(a, c, (256, 96, 128)[c] if a == 0 else 0)
-            quantise(a, 0, 512)
-            quantise(a, 512, 768)
-            if a < A - 1:
-                nc.vector.tensor_copy(slot_words[a][:], tok_words[a][:].indirect(offs_t[:]))
-        gather_bytes(0)
-        gather_words(2, 0)
-        pair(0)
-        gather_bytes(1)
-        gather_words(2, 1)
-        pair(1)
-        gather_bytes(2)
-        gather_words(2, 2)
-        last = {}
-        for m in range(M):
-            for e in (4, 5):
-                last[m, e] = psum.tile([P, PIECE], F32, name="acc")
-                for a in range(A - 1):
-                    multiply(last[m, e][:, :C], m, e, a)
-        for m in range(M):
-            for e in (4, 5):
-                multiply(last[m, e][:, :C], m, e, A - 1)
-            nc.scalar.copy(y[m][:, 4 * C : 5 * C], last[m, 4][:, :C])
-            if m == 0:
-                nc.vector.tensor_copy(y[m][:, 5 * C : 6 * C], last[m, 5][:, :C])
-            else:
-                nc.scalar.copy(y[m][:, 5 * C : 6 * C], last[m, 5][:, :C])
-
         for m in range(M):
             rows = slice(m * P, (m + 1) * P)
             first = keep.tile([P, T], F32, name=f"first{m}")
-            nc.vector.tensor_tensor(first[:], y[m][:].indirect(pos1_t[:]), gates[m][:, 0, :], MULT)
-            for t0, t1 in ((0, 512), (512, 768)) if m < M - 1 else ((0, 256), (256, 512), (512, 768)):
-                n = t1 - t0
-                second = keep.tile([P, n], F32, name=f"second{m}_{t0}")
+            second = keep.tile([P, T], F32, name=f"second{m}")
+            result = keep.tile([P, T], F32, name=f"result{m}")
+            nc.vector.tensor_tensor(first[:], y[m][:].indirect(pos1_t[:]), gates[2 * m][:], MULT)
+            for t0, t1 in ((0, 768),) if m < M - 1 else ((0, 384), (384, 768)):
                 nc.vector.tensor_tensor(
-                    second[:], y[m][:].indirect(pos2_t[:, t0 // 16 : t1 // 16]), gates[m][:, 1, t0:t1], MULT
+                    second[:, t0:t1], y[m][:].indirect(pos2_t[:, t0 // 16 : t1 // 16]), gates[2 * m + 1][:, t0:t1], MULT
                 )
-                result = keep.tile([P, n], F32, name=f"result{m}_{t0}")
-                if m == M - 1 and t0 == 512:
-                    nc.vector.tensor_tensor(result[:], first[:, t0:t1], second[:], ADD)
+            for t0, t1 in ((0, 512), (512, 768)) if m < M - 1 else ((0, 384), (384, 768)):
+                if m == M - 1 and t0 > 0:
+                    nc.vector.tensor_tensor(result[:, t0:t1], first[:, t0:t1], second[:, t0:t1], ADD)
                 else:
+                    n = t1 - t0
                     acc = psum.tile([P, PIECE], F32, name="acc")
                     nc.tensor.matmul(acc[:, :n], ident[:], first[:, t0:t1], start=True, stop=False)
-                    nc.tensor.matmul(acc[:, :n], ident[:], second[:], start=False, stop=True)
-                    nc.scalar.copy(result[:], acc[:, :n])
-                nc.sync.dma_start(out[rows, t0:t1], result[:])
+                    nc.tensor.matmul(acc[:, :n], ident[:], second[:, t0:t1], start=False, stop=True)
+                    nc.scalar.copy(result[:, t0:t1], acc[:, :n])
+                nc.sync.dma_start(out[rows, t0:t1], result[:, t0:t1])

@@ -45,10 +45,13 @@ def tile_routed_moe_kernel(tc, xT, w_words, w_scales, gate, offs, pos1, pos2, ou
 
         x_view = xT.rearrange("(a p j) t -> a p j t", p=P, j=4)
         raw = {}
+        loads = (((0, 256), (256, 512), (512, 768)), ((0, 512), (512, 768)), ((0, 512), (512, 768)))
         for a in range(A):
-            for c in range(T // CHUNK):
-                raw[a, c] = keep.tile([P, 4, CHUNK], F32, name=f"raw{a}_{c}")
-                nc.sync.dma_start(raw[a, c][:], x_view[a][:, :, c * CHUNK : (c + 1) * CHUNK])
+            for t0, t1 in loads[a]:
+                raw_at = keep.tile([P, 4, t1 - t0], F32, name=f"raw{a}_{t0}")
+                nc.sync.dma_start(raw_at[:], x_view[a][:, :, t0:t1])
+                for c in range(t0 // CHUNK, t1 // CHUNK):
+                    raw[a, c] = raw_at[:, :, c * CHUNK - t0 : (c + 1) * CHUNK - t0]
             if a == 0:
                 nc.sync.dma_start(offs_t[:], offs)
         for q in range(4):
@@ -81,11 +84,12 @@ def tile_routed_moe_kernel(tc, xT, w_words, w_scales, gate, offs, pos1, pos2, ou
 
         def interleave(a, c, share):
             base = c * CHUNK
-            src = raw[a, c][:].rearrange("p j t -> p t j")
-            if share > 0:
-                nc.vector.tensor_copy(x_bf[a][:, base : base + share, :], src[:, :share, :])
-            if share < CHUNK:
-                nc.scalar.copy(x_bf[a][:, base + share : base + CHUNK, :], src[:, share:, :])
+            for copy, t0, t1 in ((nc.vector.tensor_copy, 0, share), (nc.scalar.copy, share, CHUNK)):
+                if t0 < t1:
+                    copy(
+                        x_bf[a][:, base + t0 : base + t1, :].rearrange("p (b i) j -> p b j i", i=4),
+                        raw[a, c][:, :, t0:t1].rearrange("p j (b i) -> p b j i", i=4),
+                    )
 
         def quantise(a, t0, t1):
             nc.vector.quantize_mx(
@@ -112,7 +116,7 @@ def tile_routed_moe_kernel(tc, xT, w_words, w_scales, gate, offs, pos1, pos2, ou
 
         for a in range(A):
             for c in range(T // CHUNK):
-                interleave(a, c, (256, 96, 160)[c] if a == 0 else 0)
+                interleave(a, c, ((256, 96, 160), (0, 0, 128), (0, 0, 128))[a][c])
             quantise(a, 0, 512)
             quantise(a, 512, 768)
             if a < A - 1:

from contextlib import ExitStack

import concourse.mybir as mybir
from concourse.masks import make_identity

K, T, E, C, N = 1536, 768, 6, 256, 384
FLOPS = 2 * K * E * C * N

F32 = mybir.dt.float32
BF16 = mybir.dt.bfloat16
I32 = mybir.dt.int32
U32 = mybir.dt.uint32
U16 = mybir.dt.uint16
U8 = mybir.dt.uint8
FP8X4 = mybir.dt.float8_e4m3fn_x4
MULT = mybir.AluOpType.mult
ADD = mybir.AluOpType.add

P = 128
A = K // 512
M = N // P
CHUNK = 256
W = 2048
PIECE = 512
S = E * C // PIECE


def tile_routed_moe_kernel(tc, xT, w_words, w_scales, gate, offs, pos1, pos2, out):
    nc = tc.nc
    with ExitStack() as ctx:
        keep = ctx.enter_context(tc.tile_pool(name="keep", bufs=1))
        psum = ctx.enter_context(tc.psum_pool(name="psum", bufs=8))

        offs_t = keep.tile([P, E * C // 16], U16, name="offs_t")
        pos1_t = keep.tile([P, T // 16], U16, name="pos1_t")
        pos2_t = keep.tile([P, T // 16], U16, name="pos2_t")
        w_planes = keep.tile([P, E * A, N], U8, name="w_planes", align_bytes=64)
        tok_bytes = keep.tile([P, W], U8, name="tok_bytes", align_bytes=64)
        slot_bytes = keep.tile([P, E * C], U8, name="slot_bytes", align_bytes=64)
        ident = keep.tile([P, P], F32, name="ident")

        nc.vector.memset(w_planes[:].rearrange("p g n -> p (g n)").bitcast(I32), 0)
        nc.gpsimd.memset(tok_bytes[:, :T], 0)
        make_identity(nc, ident[:])

        x_view = xT.rearrange("(a p j) t -> a p j t", p=P, j=4)
        raw = {}
        loads = (((0, 256), (256, 512), (512, 768)), ((0, 512), (512, 768)), ((0, 512), (512, 768)))
        for a in range(A):
            for t0, t1 in loads[a]:
                raw_at = keep.tile([P, 4, t1 - t0], F32, name=f"raw{a}_{t0}")
                nc.sync.dma_start(raw_at[:], x_view[a][:, :, t0:t1])
                for c in range(t0 // CHUNK, t1 // CHUNK):
                    raw[a, c] = raw_at[:, :, c * CHUNK - t0 : (c + 1) * CHUNK - t0]
            if a == 0:
                nc.sync.dma_start(offs_t[:], offs)
        for q in range(4):
            nc.sync.dma_start(
                w_planes[32 * q : 32 * q + 4].bitcast(I32),
                w_scales.rearrange("e a q n -> q (e a) n")[4 * q : 4 * q + 4].bitcast(I32),
            )
        w = []
        for e in range(E):
            w_e = keep.tile([P, A, N], U32, name=f"w{e}", align_bytes=64)
            nc.sync.dma_start(w_e[:].bitcast(I32), w_words[e].rearrange("a p n t -> p a (n t)").bitcast(I32))
            w.append(w_e)
        nc.sync.dma_start(pos1_t[:], pos1)
        nc.sync.dma_start(pos2_t[:], pos2)
        gates = []
        for m in range(M):
            for g in range(2):
                gate_mg = keep.tile([P, T], F32, name=f"gate{m}_{g}")
                nc.sync.dma_start(gate_mg[:], gate[g, m * P : (m + 1) * P, :])
                gates.append(gate_mg)

        tok_words, slot_words, x_bf = [], [], []
        for a in range(A):
            tok_words.append(keep.tile([P, W], U32, name=f"tok_words{a}", align_bytes=64))
            slot_words.append(keep.tile([P, E * C], U32, name=f"slot_words{a}", align_bytes=64))
            x_bf.append(keep.tile([P, T, 4], BF16, name=f"x_bf{a}", align_bytes=64))
        y = []
        for m in range(M):
            y.append(keep.tile([P, E * C], F32, name=f"y{m}"))

        def interleave(a, c, share):
            base = c * CHUNK
            for copy, t0, t1 in ((nc.vector.tensor_copy, 0, share), (nc.scalar.copy, share, CHUNK)):
                if t0 < t1:
                    copy(
                        x_bf[a][:, base + t0 : base + t1, :].rearrange("p (b i) j -> p b j i", i=4),
                        raw[a, c][:, :, t0:t1].rearrange("p j (b i) -> p b j i", i=4),
                    )

        def quantise(a, t0, t1):
            nc.vector.quantize_mx(
                out=tok_words[a][:, t0:t1].bitcast(FP8X4),
                scales=tok_bytes[4 * a : P, t0:t1],
                in_=x_bf[a][:, t0:t1, :].rearrange("p t j -> p (t j)"),
            )

        def gather(dst, window, j0, j1):
            nc.vector.tensor_copy(dst[:, j0:j1], window[:].indirect(offs_t[:, j0 // 16 : j1 // 16]))

        def multiply(acc, m, e, a):
            slots = slice(e * C, (e + 1) * C)
            rows = slice(m * P, (m + 1) * P)
            nc.tensor.matmul_mx(
                out=acc,
                lhsT=w[e][:, a, rows].bitcast(FP8X4),
                lhsT_scale=w_planes[:, e * A + a, rows],
                rhs=slot_words[a][:, slots].bitcast(FP8X4),
                rhs_scale=slot_bytes[4 * a : P, slots],
                start=(a == 0),
                stop=(a == A - 1),
            )

        for a in range(A):
            for c in range(T // CHUNK):
                interleave(a, c, ((256, 96, 160), (0, 0, 128), (0, 0, 128))[a][c])
            quantise(a, 0, 512)
            quantise(a, 512, 768)
            if a < A - 1:
                gather(slot_words[a], tok_words[a], 0, E * C)
        gather(slot_bytes, tok_bytes, 0, E * C)
        gather(slot_words[2], tok_words[2], 0, 4 * C)
        gather(slot_words[2], tok_words[2], 4 * C, 6 * C)

        accs = []
        for e in range(E):
            acc = psum.tile([P, PIECE], F32, name="acc")
            for a in range(A - 1):
                multiply(acc[:, :C], 0, e, a)
            accs.append(acc)
        for e in range(E):
            multiply(accs[e][:, :C], 0, e, A - 1)
            if e == E - 1:
                nc.vector.tensor_copy(y[0][:, e * C : (e + 1) * C], accs[e][:, :C])
            else:
                nc.scalar.copy(y[0][:, e * C : (e + 1) * C], accs[e][:, :C])
        for m in range(1, M):
            for s in range(S):
                acc = psum.tile([P, PIECE], F32, name="acc")
                for h in range(2):
                    for a in range(A):
                        multiply(acc[:, h * C : (h + 1) * C], m, 2 * s + h, a)
                nc.scalar.copy(y[m][:, s * PIECE : (s + 1) * PIECE], acc[:])

        for m in range(M):
            rows = slice(m * P, (m + 1) * P)
            first = keep.tile([P, T], F32, name=f"first{m}")
            second = keep.tile([P, T], F32, name=f"second{m}")
            result = keep.tile([P, T], F32, name=f"result{m}")
            nc.vector.tensor_tensor(first[:], y[m][:].indirect(pos1_t[:]), gates[2 * m][:], MULT)
            for t0, t1 in ((0, 768),) if m < M - 1 else ((0, 384), (384, 768)):
                nc.vector.tensor_tensor(
                    second[:, t0:t1], y[m][:].indirect(pos2_t[:, t0 // 16 : t1 // 16]), gates[2 * m + 1][:, t0:t1], MULT
                )
            for t0, t1 in ((0, 512), (512, 768)) if m < M - 1 else ((0, 384), (384, 768)):
                if m == M - 1 and t0 > 0:
                    nc.vector.tensor_tensor(result[:, t0:t1], first[:, t0:t1], second[:, t0:t1], ADD)
                else:
                    n = t1 - t0
                    acc = psum.tile([P, PIECE], F32, name="acc")
                    nc.tensor.matmul(acc[:, :n], ident[:], first[:, t0:t1], start=True, stop=False)
                    nc.tensor.matmul(acc[:, :n], ident[:], second[:, t0:t1], start=False, stop=True)
                    nc.scalar.copy(result[:, t0:t1], acc[:, :n])
                nc.sync.dma_start(out[rows, t0:t1], result[:, t0:t1])
